import numpy as np
import ml_dtypes


def mxq(x, axis, fmt="e4m3"):
    dtype, down = {"e4m3": (ml_dtypes.float8_e4m3fn, 7), "e5m2": (ml_dtypes.float8_e5m2, 14)}[fmt]
    v = np.moveaxis(np.asarray(x, np.float32).astype(ml_dtypes.bfloat16).astype(np.float64), axis, -1)
    blocks = v.reshape(v.shape[:-1] + (-1, 32))
    amax = np.abs(blocks).max(-1, keepdims=True)
    byte = np.maximum(np.where(amax > 0, np.frexp(amax)[1] - 1 + 127, 0) - down, 1)
    scale = np.exp2(byte - 127.0)
    codes = (blocks / scale).astype(np.float32).astype(dtype).astype(np.float64)
    return np.moveaxis((codes * scale).reshape(v.shape), -1, axis)


WIDE = False


def mx_kscale(k):
    if not WIDE:
        return np.ones(k)
    levels = np.array([10, -10, 5, -5, 0])
    if k % 512:
        return np.exp2(np.random.permutation(np.resize(levels, k // 32))).repeat(32)
    a = np.empty((k // 512, 16))
    for p in range(k // 512):
        a[p, :8] = np.random.permutation(np.resize(levels, 8))
        for g in range(8):
            far = levels[np.abs(levels - a[p, g]) >= 10]
            a[p, g + 8] = far[np.random.randint(len(far))]
    return np.exp2(a.ravel()).repeat(32)


BF16 = ml_dtypes.bfloat16


def bf(x):
    return np.asarray(x, np.float32).astype(BF16)


def f64(x):
    return np.asarray(x).astype(np.float64)


E2M1 = np.array([0.0, 0.5, 1.0, 1.5, 2.0, 3.0, 4.0, 6.0, -0.0, -0.5, -1.0, -1.5, -2.0, -3.0, -4.0, -6.0])


def pack_weight(w, fmt):
    k, n = w.shape
    w = f64(bf(w)).reshape(k // 32, 32, n)
    amax = np.abs(w).max(1)
    if fmt == "e4m3":
        byte = np.frexp(amax)[1] - 1 + 127 - 7
    else:
        mant, ex = np.frexp(amax / 6.0)
        byte = np.where(mant > 0.5, ex, ex - 1) + 127
    byte = np.clip(np.where(amax > 0, byte, 1), 1, 254)
    scaled = (w * np.exp2(127.0 - byte)[:, None, :]).reshape(k, n).astype(np.float32)
    by_word = np.ascontiguousarray(scaled.reshape(k // 512, 128, 4, n).transpose(0, 1, 3, 2))
    if fmt == "e4m3":
        words = by_word.astype(ml_dtypes.float8_e4m3fn).view(np.uint8)
    else:
        c = by_word.astype(ml_dtypes.float4_e2m1fn).view(np.uint8) & 0xF
        words = c[..., 0::2] | (c[..., 1::2] << 4)
    return np.ascontiguousarray(words), np.ascontiguousarray(byte.astype(np.uint8).reshape(k // 512, 16, n))


def unpack_weight(words, scales, fmt):
    g, p, n, _ = words.shape
    if fmt == "e4m3":
        vals = np.ascontiguousarray(words).view(ml_dtypes.float8_e4m3fn).astype(np.float64)
    else:
        nib = np.empty((g, p, n, 4), np.uint8)
        nib[..., 0::2] = words & 0xF
        nib[..., 1::2] = words >> 4
        vals = E2M1[nib]
    vals = vals * np.repeat(np.exp2(scales.astype(np.float64) - 127.0), 8, axis=1)[..., None]
    return vals.transpose(0, 1, 3, 2).reshape(g * 512, n)
def pack4(w):
    words, scales = pack_weight(w, "e2m1")
    return words.reshape(words.shape[0], 128, -1), scales


def unpack4(words, scales):
    return unpack_weight(words.reshape(words.shape[0], 128, -1, 2), scales, "e2m1")


def planes(Y):
    n, m = Y.shape
    b = f64(bf(Y)).reshape(n // 32, 32, m)
    amax = np.abs(b).max(1)
    byte = np.clip(np.where(amax > 0, np.frexp(amax)[1] - 1 + 127 - 7, 1), 1, 254)
    codes = (b * np.exp2(127.0 - byte)[:, None, :]).reshape(n, m).astype(np.float32).astype(ml_dtypes.float8_e4m3fn).view(np.uint8)
    words = codes.reshape(n // 512, 128, 4, m).transpose(0, 1, 3, 2)
    return np.ascontiguousarray(words), np.ascontiguousarray(byte.astype(np.uint8).reshape(n // 512, 16, m))


T, D = 1536, 1024
PART_A, PART_B, PART_C = 1.0, 0.7, 0.6


def setup_inputs():
    s = mx_kscale(D)[:, None]
    psi = np.random.randn(D, T)
    size = np.exp(0.4 * np.random.randn(D))[None, :] / np.sqrt(D)
    a = PART_A * np.random.randn(D, D) * size
    b = PART_B * np.random.randn(D, D) * size
    c = PART_C * np.random.randn(D, D) * size
    psi_words, psi_scales = pack_weight(psi * s, "e4m3")
    a_words, a_scales = pack4(a / s)
    b_words, b_scales = pack_weight(b / s, "e4m3")
    rate = np.exp(0.4 * np.random.randn(T))
    return {"psi_words": psi_words, "psi_scales": psi_scales,
            "a_words": a_words, "a_scales": a_scales,
            "b_words": b_words, "b_scales": b_scales,
            "c": bf(c / s), "rate": bf(rate)}


def reference(psi_words, psi_scales, a_words, a_scales, b_words, b_scales, c, rate):
    psi = unpack_weight(psi_words, psi_scales, "e4m3").T
    ja = psi @ unpack4(a_words, a_scales)
    jb = psi @ unpack_weight(b_words, b_scales, "e4m3")
    jc = psi @ mxq(f64(c), 0, "e4m3")
    y = f64(rate)[:, None] * np.square(ja + jb + jc)
    words, scales = planes(y.T)
    return y, words, scales

@@ -1,0 +1,298 @@
+from contextlib import ExitStack
+
+import concourse.mybir as mybir
+from concourse.masks import make_identity
+
+T, D = 1536, 1024
+FLOPS = 3 * 2 * T * D * D
+
+F32 = mybir.dt.float32
+BF16 = mybir.dt.bfloat16
+I32 = mybir.dt.int32
+U32 = mybir.dt.uint32
+U8 = mybir.dt.uint8
+FP8X4 = mybir.dt.float8_e4m3fn_x4
+FP4X4 = mybir.dt.float4_e2m1fn_x4
+ACT = mybir.ActivationFunctionType
+ALU = mybir.AluOpType
+
+P = 128
+PACK = 4
+GROUP = P * PACK
+GROUPS = D // GROUP
+HALF = 512
+HALVES = D // HALF
+TILES = T // P
+CHUNK = 4
+ACC_BANKS = 6
+SCALAR_COLS = {(0, 0): 192, (0, 1): 256, (1, 0): 256, (1, 1): 256}
+
+
+def tile_lindblad_jump_populations_k3_kernel(
+    tc, psi_words, psi_scales, a_words, a_scales, b_words, b_scales, c, rate, out_0, out_1, out_2
+):
+    nc = tc.nc
+    with ExitStack() as ctx:
+        keep = ctx.enter_context(tc.tile_pool(name="keep", bufs=1))
+        work = ctx.enter_context(tc.tile_pool(name="work", bufs=4))
+        psum = ctx.enter_context(tc.psum_pool(name="psum", bufs=1))
+        ctx.enter_context(tc.manual_schedule())
+
+        def bank(index):
+            return psum.tile([P, HALF], F32, name="bank", tag="bank%d" % index)
+
+        def load_scales(queue, plane, scales):
+            rows = scales.rearrange("g (q r) n -> r q g n", r=4)
+            for r in range(4):
+                queue.dma_start(out=plane[:].bitcast(I32)[r:P:32], in_=rows[r].bitcast(I32))
+
+        psi_plane = keep.tile([P, GROUPS, T], U8, align_bytes=64)
+        a_plane = keep.tile([P, GROUPS, D], U8, align_bytes=64)
+        b_plane = keep.tile([P, GROUPS, D], U8, align_bytes=64)
+        for plane in (psi_plane, a_plane, b_plane):
+            nc.vector.memset(plane[:].bitcast(I32), 0)
+
+        rate_rows = keep.tile([P, P], BF16)
+        nc.gpsimd.memset(rate_rows[:], 0.0)
+        nc.gpsimd.dma_start(out=rate_rows[0:TILES, :], in_=rate.rearrange("(t p) -> t p", p=P))
+        identity = keep.tile([P, P], F32)
+        make_identity(nc, identity[:])
+
+        psi, a, b, c_raw = {}, {}, {}, {}
+
+        def load_psi(chunk):
+            psi[chunk] = keep.tile([P, GROUPS, CHUNK * P], U32, name="psi%d" % chunk, align_bytes=64)
+            src = psi_words.rearrange("g p n t -> p g (n t)")
+            width = CHUNK * P * PACK
+            nc.sync.dma_start(
+                out=psi[chunk][:].bitcast(I32), in_=src[:, :, chunk * width : (chunk + 1) * width].bitcast(I32)
+            )
+
+        def load_a(h):
+            a[h] = keep.tile([P, GROUPS, 2 * HALF], U8, name="a%d" % h, align_bytes=64)
+            src = a_words.rearrange("g p n -> p g n")
+            nc.sync.dma_start(
+                out=a[h][:].bitcast(I32), in_=src[:, :, h * 2 * HALF : (h + 1) * 2 * HALF].bitcast(I32)
+            )
+
+        def load_b(h):
+            b[h] = keep.tile([P, GROUPS, HALF], U32, name="b%d" % h, align_bytes=64)
+            src = b_words.rearrange("g p n t -> p g (n t)")
+            width = HALF * PACK
+            nc.sync.dma_start(out=b[h][:].bitcast(I32), in_=src[:, :, h * width : (h + 1) * width].bitcast(I32))
+
+        def load_c(h, g):
+            c_raw[h, g] = keep.tile([P, PACK, HALF], BF16, name="c_raw%d%d" % (h, g), align_bytes=64)
+            rows = c[g * GROUP : (g + 1) * GROUP, h * HALF : (h + 1) * HALF]
+            nc.sync.dma_start(out=c_raw[h, g][:], in_=rows.rearrange("(p j) n -> p j n", j=PACK))
+
+        load_psi(0)
+        load_a(0)
+        load_scales(nc.sync, psi_plane, psi_scales)
+        load_scales(nc.scalar, a_plane, a_scales)
+        load_c(0, 0)
+        load_c(0, 1)
+        load_b(0)
+        load_scales(nc.sync, b_plane, b_scales)
+        load_psi(1)
+        load_psi(2)
+        load_a(1)
+        load_c(1, 0)
+        load_c(1, 1)
+        load_b(1)
+
+        rate_rows32 = keep.tile([P, P], F32)
+        nc.scalar.copy(out=rate_rows32[:], in_=rate_rows[:])
+        rate_col = keep.tile([P, TILES], F32)
+
+        c_grouped, c_codes, c_plane = {}, {}, {}
+
+        def interleave_c(h, g):
+            c_grouped[h, g] = keep.tile([P, HALF, PACK], BF16, name="c_grouped%d%d" % (h, g), align_bytes=64)
+            split = HALF - SCALAR_COLS[h, g]
+            dst = c_grouped[h, g]
+            src = c_raw[h, g]
+            nc.vector.tensor_copy(
+                out=dst[:, 0:split, :].rearrange("p (n i) t -> p n t i", i=4),
+                in_=src[:, :, 0:split].rearrange("p t (n i) -> p n t i", i=4),
+            )
+            nc.scalar.copy(
+                out=dst[:, split:HALF, :].rearrange("p (n i) t -> p n t i", i=4),
+                in_=src[:, :, split:HALF].rearrange("p t (n i) -> p n t i", i=4),
+            )
+
+        def quantize_c(h, g):
+            c_codes[h, g] = keep.tile([P, HALF], U32, name="c_codes%d%d" % (h, g), align_bytes=64)
+            c_plane[h, g] = keep.tile([P, HALF], U8, name="c_plane%d%d" % (h, g), align_bytes=64)
+            nc.vector.quantize_mx(
+                out=c_codes[h, g][:].bitcast(FP8X4),
+                scales=c_plane[h, g][:],
+                in_=c_grouped[h, g][:].rearrange("p n t -> p (n t)"),
+            )
+
+        acc = {}
+
+        def mx_pass(unit, part, g, start=False, stop=False):
+            h, t = divmod(unit, TILES)
+            if start:
+                acc[unit] = bank(unit % ACC_BANKS)
+            cols = slice(h * HALF, (h + 1) * HALF)
+            if part == "a":
+                rhs, rhs_scale = a[h][:, g, :].bitcast(FP4X4), a_plane[:, g, cols]
+            elif part == "b":
+                rhs, rhs_scale = b[h][:, g, :].bitcast(FP8X4), b_plane[:, g, cols]
+            else:
+                rhs, rhs_scale = c_codes[h, g][:].bitcast(FP8X4), c_plane[h, g][:]
+            within = t % CHUNK
+            nc.tensor.matmul_mx(
+                out=acc[unit][:],
+                lhsT=psi[t // CHUNK][:, g, within * P : (within + 1) * P].bitcast(FP8X4),
+                lhsT_scale=psi_plane[:, g, t * P : (t + 1) * P],
+                rhs=rhs,
+                rhs_scale=rhs_scale,
+                start=start,
+                stop=stop,
+            )
+
+        def multiply(unit):
+            order = [(part, g) for part in "abc" for g in range(GROUPS)]
+            for n, (part, g) in enumerate(order):
+                mx_pass(unit, part, g, start=(n == 0), stop=(n == len(order) - 1))
+
+        y_pair, y_words = {}, {}
+
+        def finish(unit):
+            h, t = divmod(unit, TILES)
+            square = work.tile([P, HALF], F32, name="square")
+            nc.scalar.activation(out=square[:], in_=acc[unit][:], func=ACT.Square)
+            y_words[unit] = work.tile([P, 2, P, 2], BF16, name="y_words", bufs=8)
+            nc.vector.tensor_scalar(
+                out=y_words[unit][:],
+                in0=square[:].rearrange("m (p u e) -> m u p e", u=2, e=2),
+                scalar1=rate_col[:, t : t + 1],
+                scalar2=None,
+                op0=ALU.mult,
+            )
+            if unit % 2 == 0:
+                y_pair[unit // 2] = work.tile([P, 2, HALF], F32, name="y_pair")
+            nc.vector.tensor_scalar(
+                out=y_pair[unit // 2][:, unit % 2, :],
+                in0=square[:],
+                scalar1=rate_col[:, t : t + 1],
+                scalar2=None,
+                op0=ALU.mult,
+            )
+
+        def store_y(first, count):
+            h, t = divmod(first, TILES)
+            rows = out_0[t * P : (t + count) * P, h * HALF : (h + 1) * HALF]
+            nc.sync.dma_start(
+                out=rows.rearrange("(t p) n -> p t n", p=P),
+                in_=y_pair[first // 2][:, first % 2 : first % 2 + count, :],
+            )
+
+        y_codes = [keep.tile([P, T], U32, name="y_codes%d" % h, align_bytes=64) for h in range(HALVES)]
+        y_plane = [keep.tile([P, T], U8, name="y_plane%d" % h, align_bytes=64) for h in range(HALVES)]
+        turned, grouped = {}, {}
+
+        def turn(first, count, index):
+            turned[first] = bank(index)
+            view = turned[first][:].rearrange("p (t u m) -> p t u m", u=2, m=P)
+            for n in range(count):
+                words = y_words[first + n][:].rearrange("m u p e -> m (u p e)").bitcast(F32)
+                for u in range(2):
+                    nc.tensor.transpose(view[:, n, u, :], words[:, u * P : (u + 1) * P], identity[:])
+
+        def gather(first, count, dst, offset, engine_copy):
+            view = turned[first][:, 0 : count * 2 * P].rearrange("p (t u m) -> p t m u", u=2, m=P)
+            words = dst[:].bitcast(F32)[:, offset * 2 * P : (offset + count) * 2 * P]
+            engine_copy(out=words.rearrange("p (t m u) -> p t m u", u=2, m=P), in_=view)
+
+        def quantize_y(first, count, src):
+            h, t = divmod(first, TILES)
+            cols = slice(t * P, (t + count) * P)
+            nc.vector.quantize_mx(
+                out=y_codes[h][:, cols].bitcast(FP8X4), scales=y_plane[h][:, cols], in_=src[:, 0 : count * GROUP]
+            )
+
+        def store_codes(first, count, queue):
+            h, t = divmod(first, TILES)
+            dst = out_1[h].rearrange("p m t -> p (m t)")[:, t * P * PACK : (t + count) * P * PACK]
+            queue.dma_start(out=dst.bitcast(I32), in_=y_codes[h][:, t * P : (t + count) * P].bitcast(I32))
+
+        def store_scales(h, t, count, queues):
+            cols = slice(t * P, (t + count) * P)
+            for q in range(4):
+                queues[q % len(queues)].dma_start(
+                    out=out_2[h, 4 * q : 4 * q + 4, cols].bitcast(I32),
+                    in_=y_plane[h][32 * q : 32 * q + 4, cols].bitcast(I32),
+                )
+
+        def planes(first, count):
+            src = work.tile([P, CHUNK * GROUP], BF16, name="grouped", bufs=2, align_bytes=64)
+            for pair in range(count // 2):
+                gather(first + 2 * pair, 2, src, 2 * pair, nc.scalar.copy)
+            return src
+
+        for unit in range(CHUNK):
+            for g in range(GROUPS):
+                mx_pass(unit, "a", g, start=(g == 0))
+        rate_bank = bank(7)
+        nc.tensor.transpose(rate_bank[:, 0:P], rate_rows32[:], identity[:])
+        interleave_c(0, 0)
+        quantize_c(0, 0)
+        interleave_c(0, 1)
+        nc.scalar.copy(out=rate_col[:], in_=rate_bank[:, 0:TILES])
+        quantize_c(0, 1)
+        for g in range(GROUPS):
+            for unit in range(CHUNK):
+                mx_pass(unit, "c", g)
+        for unit in range(CHUNK):
+            for g in range(GROUPS):
+                mx_pass(unit, "b", g, stop=(g == GROUPS - 1))
+            finish(unit)
+            if unit % 2 == 1:
+                store_y(unit - 1, 2)
+
+        units = HALVES * TILES
+        for unit in range(CHUNK, units):
+            multiply(unit)
+            lagging = unit - CHUNK - 1
+            run = unit % CHUNK == 1 and lagging >= 0
+            if run:
+                turn(lagging, 2, 6)
+                turn(lagging + 2, 2, 7)
+            if unit == units - 2:
+                turn(units - 4, 2, 6)
+            if unit == units - 1:
+                turn(units - 2, 1, 7)
+                last_src = work.tile([P, CHUNK * GROUP], BF16, name="grouped", bufs=2, align_bytes=64)
+                gather(units - 2, 1, last_src, 0, nc.vector.tensor_copy)
+            finish(unit)
+            if unit >= units - 2:
+                store_y(unit, 1)
+            elif unit % 2 == 1:
+                store_y(unit - 1, 2)
+            if run:
+                src = planes(lagging, CHUNK)
+                quantize_y(lagging, CHUNK, src)
+                store_codes(lagging, CHUNK, nc.sync)
+                if lagging == TILES - CHUNK:
+                    store_scales(0, 0, TILES, [nc.sync])
+            if unit == units - 2:
+                src = planes(units - 4, 2)
+                quantize_y(units - 4, 2, src)
+                store_codes(units - 4, 2, nc.sync)
+                store_scales(1, 0, TILES - 2, [nc.sync])
+            if unit == 6:
+                interleave_c(1, 0)
+            if unit == 7:
+                quantize_c(1, 0)
+                interleave_c(1, 1)
+            if unit == 8:
+                quantize_c(1, 1)
+        turn(units - 1, 1, 6)
+        gather(units - 1, 1, last_src, 1, nc.scalar.copy)
+        quantize_y(units - 2, 2, last_src)
+        store_codes(units - 2, 2, nc.scalar)
+        store_scales(1, TILES - 2, 2, [nc.sync, nc.scalar])

@@ -25,7 +25,10 @@ HALVES = D // HALF
 TILES = T // P
 CHUNK = 4
 ACC_BANKS = 6
-SCALAR_COLS = {(0, 0): 192, (0, 1): 256, (1, 0): 256, (1, 1): 256}
+CHUNKS = TILES // CHUNK
+WAVE = 7
+SCALAR_COLS = {(0, 0): 192, (0, 1): 256, (1, 0): 256, (1, 1): 0}
+UNITS = [(0, t) for t in range(TILES)] + [(1, (t + CHUNK) % TILES) for t in range(TILES)]
 
 
 def tile_lindblad_jump_populations_k3_kernel(
@@ -41,31 +44,40 @@ def tile_lindblad_jump_populations_k3_kernel(
         def bank(index):
             return psum.tile([P, HALF], F32, name="bank", tag="bank%d" % index)
 
-        def load_scales(queue, plane, scales):
-            rows = scales.rearrange("g (q r) n -> r q g n", r=4)
+        def load_scales(queue, plane, scales, first, width):
+            rows = scales[:, :, first : first + width].rearrange("g (q r) n -> r q g n", r=4)
             for r in range(4):
                 queue.dma_start(out=plane[:].bitcast(I32)[r:P:32], in_=rows[r].bitcast(I32))
 
-        psi_plane = keep.tile([P, GROUPS, T], U8, align_bytes=64)
-        a_plane = keep.tile([P, GROUPS, D], U8, align_bytes=64)
+        psi_plane_first = keep.tile([P, GROUPS, CHUNK * P], U8, align_bytes=64)
+        psi_plane_rest = keep.tile([P, GROUPS, T - CHUNK * P], U8, align_bytes=64)
+        a_plane = [keep.tile([P, GROUPS, HALF], U8, name="a_plane%d" % h, align_bytes=64) for h in range(HALVES)]
         b_plane = keep.tile([P, GROUPS, D], U8, align_bytes=64)
-        for plane in (psi_plane, a_plane, b_plane):
-            nc.vector.memset(plane[:].bitcast(I32), 0)
-
-        rate_rows = keep.tile([P, P], BF16)
-        nc.gpsimd.memset(rate_rows[:], 0.0)
-        nc.gpsimd.dma_start(out=rate_rows[0:TILES, :], in_=rate.rearrange("(t p) -> t p", p=P))
-        identity = keep.tile([P, P], F32)
-        make_identity(nc, identity[:])
-
         psi, a, b, c_raw = {}, {}, {}, {}
 
-        def load_psi(chunk):
+        def load_psi(chunk, queue):
             psi[chunk] = keep.tile([P, GROUPS, CHUNK * P], U32, name="psi%d" % chunk, align_bytes=64)
             src = psi_words.rearrange("g p n t -> p g (n t)")
             width = CHUNK * P * PACK
-            nc.sync.dma_start(
+            queue.dma_start(
                 out=psi[chunk][:].bitcast(I32), in_=src[:, :, chunk * width : (chunk + 1) * width].bitcast(I32)
+            )
+
+        load_psi(0, nc.gpsimd)
+        for plane in (psi_plane_first, a_plane[0]):
+            nc.vector.memset(plane[:].bitcast(I32), 0)
+        for plane in (psi_plane_rest, b_plane, a_plane[1]):
+            nc.gpsimd.memset(plane[:].bitcast(I32), 0)
+
+        identity = keep.tile([P, P], F32)
+        make_identity(nc, identity[:])
+        rate_rows = keep.tile([P, P], BF16)
+        nc.gpsimd.memset(rate_rows[:], 0.0)
+        nc.gpsimd.dma_start(out=rate_rows[0:CHUNK, :], in_=rate[0 : CHUNK * P].rearrange("(t p) -> t p", p=P))
+        for chunk in range(1, CHUNKS):
+            nc.gpsimd.dma_start(
+                out=rate_rows[chunk * CHUNK : (chunk + 1) * CHUNK, :].rearrange("t (hi lo) -> t hi lo", lo=8),
+                in_=rate[chunk * CHUNK * P : (chunk + 1) * CHUNK * P].rearrange("(hi t lo) -> t hi lo", t=CHUNK, lo=8),
             )
 
         def load_a(h):
@@ -86,23 +98,41 @@ def tile_lindblad_jump_populations_k3_kernel(
             rows = c[g * GROUP : (g + 1) * GROUP, h * HALF : (h + 1) * HALF]
             nc.sync.dma_start(out=c_raw[h, g][:], in_=rows.rearrange("(p j) n -> p j n", j=PACK))
 
-        load_psi(0)
         load_a(0)
-        load_scales(nc.sync, psi_plane, psi_scales)
-        load_scales(nc.scalar, a_plane, a_scales)
+        load_scales(nc.sync, psi_plane_first, psi_scales, 0, CHUNK * P)
+        load_scales(nc.scalar, a_plane[0], a_scales, 0, HALF)
+        load_psi(1, nc.sync)
+        load_scales(nc.sync, psi_plane_rest, psi_scales, CHUNK * P, T - CHUNK * P)
+        load_b(0)
+        load_scales(nc.sync, b_plane, b_scales, 0, D)
         load_c(0, 0)
         load_c(0, 1)
-        load_b(0)
-        load_scales(nc.sync, b_plane, b_scales)
-        load_psi(1)
-        load_psi(2)
-        load_a(1)
+        load_psi(2, nc.sync)
         load_c(1, 0)
         load_c(1, 1)
+        load_scales(nc.sync, a_plane[1], a_scales, HALF, HALF)
+        load_a(1)
         load_b(1)
 
+        states, states_plane = {0: psi[0]}, {0: psi_plane_first}
+
+        def deal(chunk):
+            width = CHUNK * P
+            states[chunk] = keep.tile([P, GROUPS, width], U32, name="states%d" % chunk, align_bytes=64)
+            states_plane[chunk] = keep.tile([P, GROUPS, width], U8, name="states_plane%d" % chunk, align_bytes=64)
+            for g in range(GROUPS):
+                nc.vector.tensor_copy(
+                    out=states[chunk][:, g, :].bitcast(I32).rearrange("p (t hi lo) -> p t hi lo", t=CHUNK, lo=8),
+                    in_=psi[chunk][:, g, :].bitcast(I32).rearrange("p (hi t lo) -> p t hi lo", t=CHUNK, lo=8),
+                )
+            for g in range(GROUPS):
+                src = psi_plane_rest[:, g, (chunk - 1) * width : chunk * width].bitcast(I32)
+                nc.vector.tensor_copy(
+                    out=states_plane[chunk][:, g, :].bitcast(I32).rearrange("p (t hi lo) -> p t hi lo", t=CHUNK, lo=2),
+                    in_=src.rearrange("p (hi t lo) -> p t hi lo", t=CHUNK, lo=2),
+                )
+
         rate_rows32 = keep.tile([P, P], F32)
-        nc.scalar.copy(out=rate_rows32[:], in_=rate_rows[:])
         rate_col = keep.tile([P, TILES], F32)
 
         c_grouped, c_codes, c_plane = {}, {}, {}
@@ -116,10 +146,11 @@ def tile_lindblad_jump_populations_k3_kernel(
                 out=dst[:, 0:split, :].rearrange("p (n i) t -> p n t i", i=4),
                 in_=src[:, :, 0:split].rearrange("p t (n i) -> p n t i", i=4),
             )
-            nc.scalar.copy(
-                out=dst[:, split:HALF, :].rearrange("p (n i) t -> p n t i", i=4),
-                in_=src[:, :, split:HALF].rearrange("p t (n i) -> p n t i", i=4),
-            )
+            if split < HALF:
+                nc.scalar.copy(
+                    out=dst[:, split:HALF, :].rearrange("p (n i) t -> p n t i", i=4),
+                    in_=src[:, :, split:HALF].rearrange("p t (n i) -> p n t i", i=4),
+                )
 
         def quantize_c(h, g):
             c_codes[h, g] = keep.tile([P, HALF], U32, name="c_codes%d%d" % (h, g), align_bytes=64)
@@ -133,12 +164,12 @@ def tile_lindblad_jump_populations_k3_kernel(
         acc = {}
 
         def mx_pass(unit, part, g, start=False, stop=False):
-            h, t = divmod(unit, TILES)
+            h, t = UNITS[unit]
             if start:
-                acc[unit] = bank(unit % ACC_BANKS)
+                acc[unit] = bank(unit if unit < WAVE else (unit - WAVE) % ACC_BANKS)
             cols = slice(h * HALF, (h + 1) * HALF)
             if part == "a":
-                rhs, rhs_scale = a[h][:, g, :].bitcast(FP4X4), a_plane[:, g, cols]
+                rhs, rhs_scale = a[h][:, g, :].bitcast(FP4X4), a_plane[h][:, g, :]
             elif part == "b":
                 rhs, rhs_scale = b[h][:, g, :].bitcast(FP8X4), b_plane[:, g, cols]
             else:
@@ -146,8 +177,8 @@ def tile_lindblad_jump_populations_k3_kernel(
             within = t % CHUNK
             nc.tensor.matmul_mx(
                 out=acc[unit][:],
-                lhsT=psi[t // CHUNK][:, g, within * P : (within + 1) * P].bitcast(FP8X4),
-                lhsT_scale=psi_plane[:, g, t * P : (t + 1) * P],
+                lhsT=states[t // CHUNK][:, g, within * P : (within + 1) * P].bitcast(FP8X4),
+                lhsT_scale=states_plane[t // CHUNK][:, g, within * P : (within + 1) * P],
                 rhs=rhs,
                 rhs_scale=rhs_scale,
                 start=start,
@@ -162,10 +193,10 @@ def tile_lindblad_jump_populations_k3_kernel(
         y_pair, y_words = {}, {}
 
         def finish(unit):
-            h, t = divmod(unit, TILES)
-            square = work.tile([P, HALF], F32, name="square")
+            h, t = UNITS[unit]
+            square = work.tile([P, HALF], F32, name="square", bufs=8)
             nc.scalar.activation(out=square[:], in_=acc[unit][:], func=ACT.Square)
-            y_words[unit] = work.tile([P, 2, P, 2], BF16, name="y_words", bufs=8)
+            y_words[unit] = work.tile([P, 2, P, 2], BF16, name="y_words", bufs=10, align_bytes=64)
             nc.vector.tensor_scalar(
                 out=y_words[unit][:],
                 in0=square[:].rearrange("m (p u e) -> m u p e", u=2, e=2),
@@ -174,7 +205,7 @@ def tile_lindblad_jump_populations_k3_kernel(
                 op0=ALU.mult,
             )
             if unit % 2 == 0:
-                y_pair[unit // 2] = work.tile([P, 2, HALF], F32, name="y_pair")
+                y_pair[unit // 2] = work.tile([P, 2, HALF], F32, name="y_pair", bufs=6)
             nc.vector.tensor_scalar(
                 out=y_pair[unit // 2][:, unit % 2, :],
                 in0=square[:],
@@ -184,12 +215,53 @@ def tile_lindblad_jump_populations_k3_kernel(
             )
 
         def store_y(first, count):
-            h, t = divmod(first, TILES)
+            h, t = UNITS[first]
             rows = out_0[t * P : (t + count) * P, h * HALF : (h + 1) * HALF]
             nc.sync.dma_start(
                 out=rows.rearrange("(t p) n -> p t n", p=P),
                 in_=y_pair[first // 2][:, first % 2 : first % 2 + count, :],
             )
+
+        def store_dealt_y(unit):
+            h, t = UNITS[unit]
+            chunk, within = divmod(t, CHUNK)
+            rows = out_0[chunk * CHUNK * P : (chunk + 1) * CHUNK * P, h * HALF : (h + 1) * HALF]
+            nc.sync.dma_start(
+                out=rows.rearrange("(hi t lo) n -> t hi lo n", t=CHUNK, lo=8)[within],
+                in_=y_pair[unit // 2][:, unit % 2, :],
+            )
+
+        blocks, dealt_src = {}, {}
+
+        def turn_blocks(unit):
+            blocks[unit] = work.tile([P, 2 * P], F32, name="blocks", align_bytes=64)
+            nc.vector.transpose(
+                out=blocks[unit][:], in_=y_words[unit][:].rearrange("m u p e -> m (u p e)").bitcast(F32)
+            )
+
+        def gather_blocks(unit):
+            within = unit % CHUNK
+            if within == 0:
+                dealt_src[unit // CHUNK] = work.tile([P, CHUNK * GROUP], BF16, name="dealt_src", bufs=2, align_bytes=64)
+            dst = dealt_src[unit // CHUNK][:].bitcast(F32).rearrange("a (s t lo u) -> a s t lo u", t=CHUNK, lo=8, u=2)
+            nc.scalar.copy(
+                out=dst[:, :, within, :, :], in_=blocks[unit][:].rearrange("a (u s lo) -> a s lo u", u=2, lo=8)
+            )
+
+        def dealt_planes(first):
+            h, t = UNITS[first]
+            cols = slice(t * P, (t + CHUNK) * P)
+            quantize_y(first, CHUNK, dealt_src[first // CHUNK])
+            for q in (0, 2, 1, 3):
+                lo, hi = t * P + q * P, t * P + (q + 1) * P
+                dst = out_1[h].rearrange("(s a) m t -> a s (m t)", a=32)[:, :, lo * PACK : hi * PACK]
+                src = y_codes[h][32 * q : 32 * q + 32, cols].bitcast(I32)
+                nc.sync.dma_start(out=dst.bitcast(I32), in_=src.rearrange("a (s m) -> a s m", m=P))
+            for q in (0, 2, 1, 3):
+                lo, hi = t * P + q * P, t * P + (q + 1) * P
+                dst = out_2[h].rearrange("(s r) m -> r s m", r=4)[:, :, lo:hi]
+                src = y_plane[h][32 * q : 32 * q + 4, cols].bitcast(I32)
+                nc.sync.dma_start(out=dst.bitcast(I32), in_=src.rearrange("r (s m) -> r s m", s=4))
 
         y_codes = [keep.tile([P, T], U32, name="y_codes%d" % h, align_bytes=64) for h in range(HALVES)]
         y_plane = [keep.tile([P, T], U8, name="y_plane%d" % h, align_bytes=64) for h in range(HALVES)]
@@ -208,15 +280,17 @@ def tile_lindblad_jump_populations_k3_kernel(
             words = dst[:].bitcast(F32)[:, offset * 2 * P : (offset + count) * 2 * P]
             engine_copy(out=words.rearrange("p (t m u) -> p t m u", u=2, m=P), in_=view)
 
-        def quantize_y(first, count, src):
-            h, t = divmod(first, TILES)
+        def quantize_y(first, count, src, offset=0):
+            h, t = UNITS[first]
             cols = slice(t * P, (t + count) * P)
             nc.vector.quantize_mx(
-                out=y_codes[h][:, cols].bitcast(FP8X4), scales=y_plane[h][:, cols], in_=src[:, 0 : count * GROUP]
+                out=y_codes[h][:, cols].bitcast(FP8X4),
+                scales=y_plane[h][:, cols],
+                in_=src[:, offset * GROUP : (offset + count) * GROUP],
             )
 
         def store_codes(first, count, queue):
-            h, t = divmod(first, TILES)
+            h, t = UNITS[first]
             dst = out_1[h].rearrange("p m t -> p (m t)")[:, t * P * PACK : (t + count) * P * PACK]
             queue.dma_start(out=dst.bitcast(I32), in_=y_codes[h][:, t * P : (t + count) * P].bitcast(I32))
 
@@ -234,65 +308,78 @@ def tile_lindblad_jump_populations_k3_kernel(
                 gather(first + 2 * pair, 2, src, 2 * pair, nc.scalar.copy)
             return src
 
-        for unit in range(CHUNK):
+        units = len(UNITS)
+
+        def dealt(unit):
+            return UNITS[unit][1] >= CHUNK
+
+        def after(unit):
+            closes = unit > 0 and dealt(unit - 1) and unit % CHUNK == 0
+            if closes:
+                gather_blocks(unit - 1)
+                dealt_planes(unit - CHUNK)
+            finish(unit)
+            if dealt(unit):
+                turn_blocks(unit)
+                store_dealt_y(unit)
+            elif unit >= units - 2:
+                store_y(unit, 1)
+            elif unit % 2 == 1:
+                store_y(unit - 1, 2)
+            if unit > 0 and dealt(unit - 1) and not closes:
+                gather_blocks(unit - 1)
+
+        deal(1)
+        for unit in range(WAVE):
             for g in range(GROUPS):
                 mx_pass(unit, "a", g, start=(g == 0))
-        rate_bank = bank(7)
-        nc.tensor.transpose(rate_bank[:, 0:P], rate_rows32[:], identity[:])
+        for unit in range(WAVE):
+            for g in range(GROUPS):
+                mx_pass(unit, "b", g)
         interleave_c(0, 0)
         quantize_c(0, 0)
         interleave_c(0, 1)
-        nc.scalar.copy(out=rate_col[:], in_=rate_bank[:, 0:TILES])
         quantize_c(0, 1)
-        for g in range(GROUPS):
-            for unit in range(CHUNK):
-                mx_pass(unit, "c", g)
-        for unit in range(CHUNK):
-            for g in range(GROUPS):
-                mx_pass(unit, "b", g, stop=(g == GROUPS - 1))
-            finish(unit)
-            if unit % 2 == 1:
-                store_y(unit - 1, 2)
+        nc.scalar.copy(out=rate_rows32[:], in_=rate_rows[:])
+        rate_bank = bank(7)
+        nc.tensor.transpose(rate_bank[:, 0:P], rate_rows32[:], identity[:])
+        nc.scalar.copy(out=rate_col[:], in_=rate_bank[:, 0:TILES])
+        deal(2)
+        interleave_c(1, 0)
+        quantize_c(1, 0)
+        interleave_c(1, 1)
+        quantize_c(1, 1)
+        for unit in range(WAVE):
+            mx_pass(unit, "c", 0)
+        for unit in range(WAVE):
+            mx_pass(unit, "c", 1, stop=True)
+            after(unit)
 
-        units = HALVES * TILES
-        for unit in range(CHUNK, units):
+        for unit in range(WAVE, units):
             multiply(unit)
-            lagging = unit - CHUNK - 1
-            run = unit % CHUNK == 1 and lagging >= 0
-            if run:
-                turn(lagging, 2, 6)
-                turn(lagging + 2, 2, 7)
+            if unit == WAVE + 1:
+                turn(0, 2, 7)
+                turn(2, 2, 6)
             if unit == units - 2:
                 turn(units - 4, 2, 6)
             if unit == units - 1:
                 turn(units - 2, 1, 7)
                 last_src = work.tile([P, CHUNK * GROUP], BF16, name="grouped", bufs=2, align_bytes=64)
                 gather(units - 2, 1, last_src, 0, nc.vector.tensor_copy)
-            finish(unit)
-            if unit >= units - 2:
-                store_y(unit, 1)
-            elif unit % 2 == 1:
-                store_y(unit - 1, 2)
-            if run:
-                src = planes(lagging, CHUNK)
-                quantize_y(lagging, CHUNK, src)
-                store_codes(lagging, CHUNK, nc.sync)
-                if lagging == TILES - CHUNK:
-                    store_scales(0, 0, TILES, [nc.sync])
+            after(unit)
+            if unit == WAVE + 1:
+                src = planes(0, CHUNK)
+            if unit == WAVE + 2:
+                quantize_y(0, CHUNK, src)
+                store_codes(0, CHUNK, nc.sync)
+                store_scales(0, 0, CHUNK, [nc.sync])
             if unit == units - 2:
                 src = planes(units - 4, 2)
                 quantize_y(units - 4, 2, src)
                 store_codes(units - 4, 2, nc.sync)
-                store_scales(1, 0, TILES - 2, [nc.sync])
-            if unit == 6:
-                interleave_c(1, 0)
-            if unit == 7:
-                quantize_c(1, 0)
-                interleave_c(1, 1)
-            if unit == 8:
-                quantize_c(1, 1)
+        quantize_y(units - 2, 1, last_src)
         turn(units - 1, 1, 6)
         gather(units - 1, 1, last_src, 1, nc.scalar.copy)
-        quantize_y(units - 2, 2, last_src)
+        quantize_y(units - 1, 1, last_src, 1)
         store_codes(units - 2, 2, nc.scalar)
-        store_scales(1, TILES - 2, 2, [nc.sync, nc.scalar])
+        store_scales(1, 0, CHUNK, [nc.sync, nc.scalar])

@@ -27,8 +27,10 @@ CHUNK = 4
 ACC_BANKS = 6
 CHUNKS = TILES // CHUNK
 WAVE = 7
-SCALAR_COLS = {(0, 0): 192, (0, 1): 256, (1, 0): 256, (1, 1): 0}
-UNITS = [(0, t) for t in range(TILES)] + [(1, (t + CHUNK) % TILES) for t in range(TILES)]
+SCALAR_COLS = {(0, 0): 192, (0, 1): 256, (1, 0): 192, (1, 1): 192}
+CHUNK_ORDER = ((0, 0), (0, 1), (0, 2), (1, 0), (1, 1), (1, 2))
+DEALT = ()
+UNITS = [(h, chunk * CHUNK + n) for h, chunk in CHUNK_ORDER for n in range(CHUNK)]
 
 
 def tile_lindblad_jump_populations_k3_kernel(
@@ -51,7 +53,7 @@ def tile_lindblad_jump_populations_k3_kernel(
 
         psi_plane_first = keep.tile([P, GROUPS, CHUNK * P], U8, align_bytes=64)
         psi_plane_rest = keep.tile([P, GROUPS, T - CHUNK * P], U8, align_bytes=64)
-        a_plane = [keep.tile([P, GROUPS, HALF], U8, name="a_plane%d" % h, align_bytes=64) for h in range(HALVES)]
+        a_plane = keep.tile([P, GROUPS, D], U8, align_bytes=64)
         b_plane = keep.tile([P, GROUPS, D], U8, align_bytes=64)
         psi, a, b, c_raw = {}, {}, {}, {}
 
@@ -63,22 +65,14 @@ def tile_lindblad_jump_populations_k3_kernel(
                 out=psi[chunk][:].bitcast(I32), in_=src[:, :, chunk * width : (chunk + 1) * width].bitcast(I32)
             )
 
-        load_psi(0, nc.gpsimd)
-        for plane in (psi_plane_first, a_plane[0]):
+        for plane in (psi_plane_first, a_plane, psi_plane_rest, b_plane):
             nc.vector.memset(plane[:].bitcast(I32), 0)
-        for plane in (psi_plane_rest, b_plane, a_plane[1]):
-            nc.gpsimd.memset(plane[:].bitcast(I32), 0)
 
-        identity = keep.tile([P, P], F32)
-        make_identity(nc, identity[:])
         rate_rows = keep.tile([P, P], BF16)
         nc.gpsimd.memset(rate_rows[:], 0.0)
-        nc.gpsimd.dma_start(out=rate_rows[0:CHUNK, :], in_=rate[0 : CHUNK * P].rearrange("(t p) -> t p", p=P))
-        for chunk in range(1, CHUNKS):
-            nc.gpsimd.dma_start(
-                out=rate_rows[chunk * CHUNK : (chunk + 1) * CHUNK, :].rearrange("t (hi lo) -> t hi lo", lo=8),
-                in_=rate[chunk * CHUNK * P : (chunk + 1) * CHUNK * P].rearrange("(hi t lo) -> t hi lo", t=CHUNK, lo=8),
-            )
+        nc.gpsimd.dma_start(out=rate_rows[0:TILES, :], in_=rate.rearrange("(t p) -> t p", p=P))
+        identity = keep.tile([P, P], F32)
+        make_identity(nc, identity[:])
 
         def load_a(h):
             a[h] = keep.tile([P, GROUPS, 2 * HALF], U8, name="a%d" % h, align_bytes=64)
@@ -98,23 +92,27 @@ def tile_lindblad_jump_populations_k3_kernel(
             rows = c[g * GROUP : (g + 1) * GROUP, h * HALF : (h + 1) * HALF]
             nc.sync.dma_start(out=c_raw[h, g][:], in_=rows.rearrange("(p j) n -> p j n", j=PACK))
 
-        load_a(0)
+        load_c(0, 0)
+        load_psi(0, nc.sync)
         load_scales(nc.sync, psi_plane_first, psi_scales, 0, CHUNK * P)
-        load_scales(nc.scalar, a_plane[0], a_scales, 0, HALF)
+        load_a(0)
+        load_scales(nc.sync, a_plane, a_scales, 0, D)
         load_psi(1, nc.sync)
         load_scales(nc.sync, psi_plane_rest, psi_scales, CHUNK * P, T - CHUNK * P)
         load_b(0)
         load_scales(nc.sync, b_plane, b_scales, 0, D)
-        load_c(0, 0)
         load_c(0, 1)
         load_psi(2, nc.sync)
         load_c(1, 0)
         load_c(1, 1)
-        load_scales(nc.sync, a_plane[1], a_scales, HALF, HALF)
         load_a(1)
         load_b(1)
 
-        states, states_plane = {0: psi[0]}, {0: psi_plane_first}
+        states, states_plane = {}, {}
+
+        def dealt(unit):
+            h, t = UNITS[unit]
+            return (h, t // CHUNK) in DEALT
 
         def deal(chunk):
             width = CHUNK * P
@@ -122,18 +120,18 @@ def tile_lindblad_jump_populations_k3_kernel(
             states_plane[chunk] = keep.tile([P, GROUPS, width], U8, name="states_plane%d" % chunk, align_bytes=64)
             for g in range(GROUPS):
                 nc.vector.tensor_copy(
-                    out=states[chunk][:, g, :].bitcast(I32).rearrange("p (t hi lo) -> p t hi lo", t=CHUNK, lo=8),
-                    in_=psi[chunk][:, g, :].bitcast(I32).rearrange("p (hi t lo) -> p t hi lo", t=CHUNK, lo=8),
+                    out=states[chunk][:, g, :].bitcast(I32).rearrange("p (t x i) -> p x t i", t=CHUNK, i=4),
+                    in_=psi[chunk][:, g, :].bitcast(I32).rearrange("p (x i t) -> p x t i", t=CHUNK, i=4),
                 )
             for g in range(GROUPS):
-                src = psi_plane_rest[:, g, (chunk - 1) * width : chunk * width].bitcast(I32)
+                src = psi_plane_rest[:, g, (chunk - 1) * width : chunk * width]
                 nc.vector.tensor_copy(
-                    out=states_plane[chunk][:, g, :].bitcast(I32).rearrange("p (t hi lo) -> p t hi lo", t=CHUNK, lo=2),
-                    in_=src.rearrange("p (hi t lo) -> p t hi lo", t=CHUNK, lo=2),
+                    out=states_plane[chunk][:, g, :].rearrange("p (t x i) -> p x t i", t=CHUNK, i=16),
+                    in_=src.rearrange("p (x i t) -> p x t i", t=CHUNK, i=16),
                 )
 
         rate_rows32 = keep.tile([P, P], F32)
-        rate_col = keep.tile([P, TILES], F32)
+        rate_col = keep.tile([P, 2, TILES], F32)
 
         c_grouped, c_codes, c_plane = {}, {}, {}
 
@@ -169,16 +167,23 @@ def tile_lindblad_jump_populations_k3_kernel(
                 acc[unit] = bank(unit if unit < WAVE else (unit - WAVE) % ACC_BANKS)
             cols = slice(h * HALF, (h + 1) * HALF)
             if part == "a":
-                rhs, rhs_scale = a[h][:, g, :].bitcast(FP4X4), a_plane[h][:, g, :]
+                rhs, rhs_scale = a[h][:, g, :].bitcast(FP4X4), a_plane[:, g, cols]
             elif part == "b":
                 rhs, rhs_scale = b[h][:, g, :].bitcast(FP8X4), b_plane[:, g, cols]
             else:
                 rhs, rhs_scale = c_codes[h, g][:].bitcast(FP8X4), c_plane[h, g][:]
-            within = t % CHUNK
+            chunk, within = divmod(t, CHUNK)
+            own = slice(within * P, (within + 1) * P)
+            if dealt(unit):
+                lhs, lhs_scale = states[chunk][:, g, own], states_plane[chunk][:, g, own]
+            elif chunk == 0:
+                lhs, lhs_scale = psi[chunk][:, g, own], psi_plane_first[:, g, own]
+            else:
+                lhs, lhs_scale = psi[chunk][:, g, own], psi_plane_rest[:, g, (t - CHUNK) * P : (t - CHUNK + 1) * P]
             nc.tensor.matmul_mx(
                 out=acc[unit][:],
-                lhsT=states[t // CHUNK][:, g, within * P : (within + 1) * P].bitcast(FP8X4),
-                lhsT_scale=states_plane[t // CHUNK][:, g, within * P : (within + 1) * P],
+                lhsT=lhs.bitcast(FP8X4),
+                lhsT_scale=lhs_scale,
                 rhs=rhs,
                 rhs_scale=rhs_scale,
                 start=start,
@@ -194,13 +199,14 @@ def tile_lindblad_jump_populations_k3_kernel(
 
         def finish(unit):
             h, t = UNITS[unit]
+            factor = rate_col[:, int(dealt(unit)), t : t + 1]
             square = work.tile([P, HALF], F32, name="square", bufs=8)
             nc.scalar.activation(out=square[:], in_=acc[unit][:], func=ACT.Square)
             y_words[unit] = work.tile([P, 2, P, 2], BF16, name="y_words", bufs=10, align_bytes=64)
             nc.vector.tensor_scalar(
                 out=y_words[unit][:],
                 in0=square[:].rearrange("m (p u e) -> m u p e", u=2, e=2),
-                scalar1=rate_col[:, t : t + 1],
+                scalar1=factor,
                 scalar2=None,
                 op0=ALU.mult,
             )
@@ -209,7 +215,30 @@ def tile_lindblad_jump_populations_k3_kernel(
             nc.vector.tensor_scalar(
                 out=y_pair[unit // 2][:, unit % 2, :],
                 in0=square[:],
-                scalar1=rate_col[:, t : t + 1],
+                scalar1=factor,
+                scalar2=None,
+                op0=ALU.mult,
+            )
+
+        def finish_last(unit):
+            h, t = UNITS[unit]
+            factor = rate_col[:, 0, t : t + 1]
+            square = work.tile([P, HALF], F32, name="square", bufs=8)
+            halves = square[:].rearrange("m (u p e) -> m u p e", u=2, e=2)
+            y_words[unit] = work.tile([P, 2, P, 2], BF16, name="y_words", bufs=10, align_bytes=64)
+            for u in range(2):
+                nc.scalar.activation(
+                    out=halves[:, u],
+                    in_=acc[unit][:].rearrange("m (p u e) -> m u p e", u=2, e=2)[:, u],
+                    func=ACT.Square,
+                )
+                nc.vector.tensor_scalar(
+                    out=y_words[unit][:, u], in0=halves[:, u], scalar1=factor, scalar2=None, op0=ALU.mult
+                )
+            nc.vector.tensor_scalar(
+                out=y_pair[unit // 2][:, unit % 2, :].rearrange("m (p u e) -> m p u e", u=2, e=2),
+                in0=square[:].rearrange("m (u p e) -> m p u e", u=2, e=2),
+                scalar1=factor,
                 scalar2=None,
                 op0=ALU.mult,
             )
@@ -222,47 +251,61 @@ def tile_lindblad_jump_populations_k3_kernel(
                 in_=y_pair[first // 2][:, first % 2 : first % 2 + count, :],
             )
 
-        def store_dealt_y(unit):
-            h, t = UNITS[unit]
+        def store_dealt_y(first):
+            h, t = UNITS[first]
             chunk, within = divmod(t, CHUNK)
             rows = out_0[chunk * CHUNK * P : (chunk + 1) * CHUNK * P, h * HALF : (h + 1) * HALF]
             nc.sync.dma_start(
-                out=rows.rearrange("(hi t lo) n -> t hi lo n", t=CHUNK, lo=8)[within],
-                in_=y_pair[unit // 2][:, unit % 2, :],
+                out=rows.rearrange("(p t) n -> p t n", t=CHUNK)[:, within : within + 2, :],
+                in_=y_pair[first // 2][:],
             )
 
-        blocks, dealt_src = {}, {}
+        blocks, dealt_src, waiting = {}, {}, {}
 
         def turn_blocks(unit):
-            blocks[unit] = work.tile([P, 2 * P], F32, name="blocks", align_bytes=64)
+            if unit % 2 == 0:
+                blocks[unit // 2] = work.tile([P, 2, 2 * P], F32, name="blocks", bufs=3, align_bytes=64)
             nc.vector.transpose(
-                out=blocks[unit][:], in_=y_words[unit][:].rearrange("m u p e -> m (u p e)").bitcast(F32)
+                out=blocks[unit // 2][:, unit % 2, :],
+                in_=y_words[unit][:].rearrange("m u p e -> m (u p e)").bitcast(F32),
             )
 
-        def gather_blocks(unit):
-            within = unit % CHUNK
+        def gather_blocks(first):
+            within = first % CHUNK
             if within == 0:
-                dealt_src[unit // CHUNK] = work.tile([P, CHUNK * GROUP], BF16, name="dealt_src", bufs=2, align_bytes=64)
-            dst = dealt_src[unit // CHUNK][:].bitcast(F32).rearrange("a (s t lo u) -> a s t lo u", t=CHUNK, lo=8, u=2)
+                dealt_src[first // CHUNK] = work.tile([P, CHUNK * GROUP], BF16, name="dealt_src", bufs=2, align_bytes=64)
+            dst = dealt_src[first // CHUNK][:].bitcast(F32).rearrange("a (x t u) -> a x t u", t=CHUNK, u=2)
             nc.scalar.copy(
-                out=dst[:, :, within, :, :], in_=blocks[unit][:].rearrange("a (u s lo) -> a s lo u", u=2, lo=8)
+                out=dst[:, :, within : within + 2, :], in_=blocks[first // 2][:].rearrange("a t (u x) -> a x t u", u=2)
             )
 
         def dealt_planes(first):
             h, t = UNITS[first]
-            cols = slice(t * P, (t + CHUNK) * P)
-            quantize_y(first, CHUNK, dealt_src[first // CHUNK])
-            for q in (0, 2, 1, 3):
-                lo, hi = t * P + q * P, t * P + (q + 1) * P
-                dst = out_1[h].rearrange("(s a) m t -> a s (m t)", a=32)[:, :, lo * PACK : hi * PACK]
-                src = y_codes[h][32 * q : 32 * q + 32, cols].bitcast(I32)
-                nc.sync.dma_start(out=dst.bitcast(I32), in_=src.rearrange("a (s m) -> a s m", m=P))
-            for q in (0, 2, 1, 3):
-                lo, hi = t * P + q * P, t * P + (q + 1) * P
-                dst = out_2[h].rearrange("(s r) m -> r s m", r=4)[:, :, lo:hi]
-                src = y_plane[h][32 * q : 32 * q + 4, cols].bitcast(I32)
-                nc.sync.dma_start(out=dst.bitcast(I32), in_=src.rearrange("r (s m) -> r s m", s=4))
+            for s in range(4):
+                nc.vector.quantize_mx(
+                    out=y_codes[h][:, (t + s) * P : (t + s + 1) * P].bitcast(FP8X4),
+                    scales=dealt_plane[h][4 * s : P, t // CHUNK - 1, :],
+                    in_=dealt_src[first // CHUNK][:, s * GROUP : (s + 1) * GROUP],
+                )
+            for s in range(4):
+                dst = out_1[h, 32 * s : 32 * s + 32, t * P : (t + CHUNK) * P, :]
+                nc.sync.dma_start(
+                    out=dst.rearrange("a (q m) t -> q a (m t)", q=4).bitcast(I32),
+                    in_=y_codes[h][:, (t + s) * P : (t + s + 1) * P].bitcast(I32),
+                )
+            count = t // CHUNK
+            if (h, count + 1) not in DEALT:
+                for n, q in enumerate((0, 2, 1, 3)):
+                    waiting.setdefault(first + CHUNK + max(0, 2 * n - 1), []).append((h, q, count))
 
+        def store_waiting_scales(unit):
+            for h, q, count in waiting.get(unit, []):
+                dst = out_2[h, :, CHUNK * P : (count + 1) * CHUNK * P].rearrange("j (c q m) -> q j c m", q=4, m=P)[q]
+                nc.sync.dma_start(out=dst.bitcast(I32), in_=dealt_plane[h][32 * q : 32 * q + 16, 0:count, :].bitcast(I32))
+
+        dealt_plane = [
+            keep.tile([P, CHUNKS - 1, P], U8, name="dealt_plane%d" % h, align_bytes=64) for h in range(HALVES)
+        ]
         y_codes = [keep.tile([P, T], U32, name="y_codes%d" % h, align_bytes=64) for h in range(HALVES)]
         y_plane = [keep.tile([P, T], U8, name="y_plane%d" % h, align_bytes=64) for h in range(HALVES)]
         turned, grouped = {}, {}
@@ -310,56 +353,54 @@ def tile_lindblad_jump_populations_k3_kernel(
 
         units = len(UNITS)
 
-        def dealt(unit):
-            return UNITS[unit][1] >= CHUNK
-
         def after(unit):
-            closes = unit > 0 and dealt(unit - 1) and unit % CHUNK == 0
-            if closes:
-                gather_blocks(unit - 1)
+            if unit > 0 and dealt(unit - 1) and unit % CHUNK == 0:
+                gather_blocks(unit - 2)
                 dealt_planes(unit - CHUNK)
-            finish(unit)
+            if unit == units - 1:
+                finish_last(unit)
+            else:
+                finish(unit)
             if dealt(unit):
                 turn_blocks(unit)
-                store_dealt_y(unit)
+                if unit % 2 == 1:
+                    store_dealt_y(unit - 1)
+                if unit % CHUNK == 2:
+                    gather_blocks(unit - 2)
             elif unit >= units - 2:
                 store_y(unit, 1)
             elif unit % 2 == 1:
                 store_y(unit - 1, 2)
-            if unit > 0 and dealt(unit - 1) and not closes:
-                gather_blocks(unit - 1)
+            store_waiting_scales(unit)
 
-        deal(1)
-        for unit in range(WAVE):
-            for g in range(GROUPS):
-                mx_pass(unit, "a", g, start=(g == 0))
-        for unit in range(WAVE):
-            for g in range(GROUPS):
-                mx_pass(unit, "b", g)
         interleave_c(0, 0)
         quantize_c(0, 0)
-        interleave_c(0, 1)
-        quantize_c(0, 1)
+        for first, last in ((0, CHUNK), (CHUNK, WAVE)):
+            for unit in range(first, last):
+                mx_pass(unit, "c", 0, start=True)
+            for unit in range(first, last):
+                for g in range(GROUPS):
+                    mx_pass(unit, "a", g)
         nc.scalar.copy(out=rate_rows32[:], in_=rate_rows[:])
         rate_bank = bank(7)
         nc.tensor.transpose(rate_bank[:, 0:P], rate_rows32[:], identity[:])
-        nc.scalar.copy(out=rate_col[:], in_=rate_bank[:, 0:TILES])
-        deal(2)
-        interleave_c(1, 0)
-        quantize_c(1, 0)
-        interleave_c(1, 1)
-        quantize_c(1, 1)
+        nc.scalar.copy(out=rate_col[:, 0, :], in_=rate_bank[:, 0:TILES])
         for unit in range(WAVE):
-            mx_pass(unit, "c", 0)
+            for g in range(GROUPS):
+                mx_pass(unit, "b", g)
+        for h, g in ((0, 1), (1, 0), (1, 1)):
+            interleave_c(h, g)
+            quantize_c(h, g)
         for unit in range(WAVE):
             mx_pass(unit, "c", 1, stop=True)
             after(unit)
 
+        runs = {8: 0, 10: 4, 13: 8, 17: 12, 20: 16}
         for unit in range(WAVE, units):
             multiply(unit)
-            if unit == WAVE + 1:
-                turn(0, 2, 7)
-                turn(2, 2, 6)
+            if unit in runs:
+                turn(runs[unit], 2, 7)
+                turn(runs[unit] + 2, 2, 6)
             if unit == units - 2:
                 turn(units - 4, 2, 6)
             if unit == units - 1:
@@ -367,12 +408,14 @@ def tile_lindblad_jump_populations_k3_kernel(
                 last_src = work.tile([P, CHUNK * GROUP], BF16, name="grouped", bufs=2, align_bytes=64)
                 gather(units - 2, 1, last_src, 0, nc.vector.tensor_copy)
             after(unit)
-            if unit == WAVE + 1:
-                src = planes(0, CHUNK)
-            if unit == WAVE + 2:
-                quantize_y(0, CHUNK, src)
-                store_codes(0, CHUNK, nc.sync)
-                store_scales(0, 0, CHUNK, [nc.sync])
+            if unit in runs:
+                src = planes(runs[unit], CHUNK)
+                quantize_y(runs[unit], CHUNK, src)
+                store_codes(runs[unit], CHUNK, nc.sync)
+                if runs[unit] == 8:
+                    store_scales(0, 0, TILES, [nc.sync])
+                if runs[unit] == 16:
+                    store_scales(1, 0, TILES - CHUNK, [nc.sync])
             if unit == units - 2:
                 src = planes(units - 4, 2)
                 quantize_y(units - 4, 2, src)
@@ -382,4 +425,4 @@ def tile_lindblad_jump_populations_k3_kernel(
         gather(units - 1, 1, last_src, 1, nc.scalar.copy)
         quantize_y(units - 1, 1, last_src, 1)
         store_codes(units - 2, 2, nc.scalar)
-        store_scales(1, 0, CHUNK, [nc.sync, nc.scalar])
+        store_scales(1, TILES - CHUNK, CHUNK, [nc.sync, nc.scalar])

from contextlib import ExitStack

import concourse.mybir as mybir
from concourse.masks import make_identity

T, D = 1536, 1024
FLOPS = 3 * 2 * T * D * D

F32 = mybir.dt.float32
BF16 = mybir.dt.bfloat16
I32 = mybir.dt.int32
U32 = mybir.dt.uint32
U8 = mybir.dt.uint8
FP8X4 = mybir.dt.float8_e4m3fn_x4
FP4X4 = mybir.dt.float4_e2m1fn_x4
ACT = mybir.ActivationFunctionType
ALU = mybir.AluOpType

P = 128
PACK = 4
GROUP = P * PACK
GROUPS = D // GROUP
HALF = 512
HALVES = D // HALF
TILES = T // P
CHUNK = 4
ACC_BANKS = 6
CHUNKS = TILES // CHUNK
WAVE = 7
SCALAR_COLS = {(0, 0): 192, (0, 1): 256, (1, 0): 192, (1, 1): 192}
CHUNK_ORDER = ((0, 0), (0, 1), (0, 2), (1, 0), (1, 1), (1, 2))
DEALT = ()
UNITS = [(h, chunk * CHUNK + n) for h, chunk in CHUNK_ORDER for n in range(CHUNK)]


def tile_lindblad_jump_populations_k3_kernel(
    tc, psi_words, psi_scales, a_words, a_scales, b_words, b_scales, c, rate, out_0, out_1, out_2
):
    nc = tc.nc
    with ExitStack() as ctx:
        keep = ctx.enter_context(tc.tile_pool(name="keep", bufs=1))
        work = ctx.enter_context(tc.tile_pool(name="work", bufs=4))
        psum = ctx.enter_context(tc.psum_pool(name="psum", bufs=1))
        ctx.enter_context(tc.manual_schedule())

        def bank(index):
            return psum.tile([P, HALF], F32, name="bank", tag="bank%d" % index)

        def load_scales(queue, plane, scales, first, width):
            rows = scales[:, :, first : first + width].rearrange("g (q r) n -> r q g n", r=4)
            for r in range(4):
                queue.dma_start(out=plane[:].bitcast(I32)[r:P:32], in_=rows[r].bitcast(I32))

        psi_plane_first = keep.tile([P, GROUPS, CHUNK * P], U8, align_bytes=64)
        psi_plane_rest = keep.tile([P, GROUPS, T - CHUNK * P], U8, align_bytes=64)
        a_plane = keep.tile([P, GROUPS, D], U8, align_bytes=64)
        b_plane = keep.tile([P, GROUPS, D], U8, align_bytes=64)
        psi, a, b, c_raw = {}, {}, {}, {}

        def load_psi(chunk, queue):
            psi[chunk] = keep.tile([P, GROUPS, CHUNK * P], U32, name="psi%d" % chunk, align_bytes=64)
            src = psi_words.rearrange("g p n t -> p g (n t)")
            width = CHUNK * P * PACK
            queue.dma_start(
                out=psi[chunk][:].bitcast(I32), in_=src[:, :, chunk * width : (chunk + 1) * width].bitcast(I32)
            )

        for plane in (psi_plane_first, a_plane, psi_plane_rest, b_plane):
            nc.vector.memset(plane[:].bitcast(I32), 0)

        rate_rows = keep.tile([P, P], BF16)
        nc.gpsimd.memset(rate_rows[:], 0.0)
        nc.gpsimd.dma_start(out=rate_rows[0:TILES, :], in_=rate.rearrange("(t p) -> t p", p=P))
        identity = keep.tile([P, P], F32)
        make_identity(nc, identity[:])

        def load_a(h):
            a[h] = keep.tile([P, GROUPS, 2 * HALF], U8, name="a%d" % h, align_bytes=64)
            src = a_words.rearrange("g p n -> p g n")
            nc.sync.dma_start(
                out=a[h][:].bitcast(I32), in_=src[:, :, h * 2 * HALF : (h + 1) * 2 * HALF].bitcast(I32)
            )

        def load_b(h):
            b[h] = keep.tile([P, GROUPS, HALF], U32, name="b%d" % h, align_bytes=64)
            src = b_words.rearrange("g p n t -> p g (n t)")
            width = HALF * PACK
            nc.sync.dma_start(out=b[h][:].bitcast(I32), in_=src[:, :, h * width : (h + 1) * width].bitcast(I32))

        def load_c(h, g):
            c_raw[h, g] = keep.tile([P, PACK, HALF], BF16, name="c_raw%d%d" % (h, g), align_bytes=64)
            rows = c[g * GROUP : (g + 1) * GROUP, h * HALF : (h + 1) * HALF]
            nc.sync.dma_start(out=c_raw[h, g][:], in_=rows.rearrange("(p j) n -> p j n", j=PACK))

        load_c(0, 0)
        load_psi(0, nc.sync)
        load_scales(nc.sync, psi_plane_first, psi_scales, 0, CHUNK * P)
        load_a(0)
        load_scales(nc.sync, a_plane, a_scales, 0, D)
        load_psi(1, nc.sync)
        load_scales(nc.sync, psi_plane_rest, psi_scales, CHUNK * P, T - CHUNK * P)
        load_b(0)
        load_scales(nc.sync, b_plane, b_scales, 0, D)
        load_c(0, 1)
        load_psi(2, nc.sync)
        load_c(1, 0)
        load_c(1, 1)
        load_a(1)
        load_b(1)

        states, states_plane = {}, {}

        def dealt(unit):
            h, t = UNITS[unit]
            return (h, t // CHUNK) in DEALT

        def deal(chunk):
            width = CHUNK * P
            states[chunk] = keep.tile([P, GROUPS, width], U32, name="states%d" % chunk, align_bytes=64)
            states_plane[chunk] = keep.tile([P, GROUPS, width], U8, name="states_plane%d" % chunk, align_bytes=64)
            for g in range(GROUPS):
                nc.vector.tensor_copy(
                    out=states[chunk][:, g, :].bitcast(I32).rearrange("p (t x i) -> p x t i", t=CHUNK, i=4),
                    in_=psi[chunk][:, g, :].bitcast(I32).rearrange("p (x i t) -> p x t i", t=CHUNK, i=4),
                )
            for g in range(GROUPS):
                src = psi_plane_rest[:, g, (chunk - 1) * width : chunk * width]
                nc.vector.tensor_copy(
                    out=states_plane[chunk][:, g, :].rearrange("p (t x i) -> p x t i", t=CHUNK, i=16),
                    in_=src.rearrange("p (x i t) -> p x t i", t=CHUNK, i=16),
                )

        rate_rows32 = keep.tile([P, P], F32)
        rate_col = keep.tile([P, 2, TILES], F32)

        c_grouped, c_codes, c_plane = {}, {}, {}

        def interleave_c(h, g):
            c_grouped[h, g] = keep.tile([P, HALF, PACK], BF16, name="c_grouped%d%d" % (h, g), align_bytes=64)
            split = HALF - SCALAR_COLS[h, g]
            dst = c_grouped[h, g]
            src = c_raw[h, g]
            nc.vector.tensor_copy(
                out=dst[:, 0:split, :].rearrange("p (n i) t -> p n t i", i=4),
                in_=src[:, :, 0:split].rearrange("p t (n i) -> p n t i", i=4),
            )
            if split < HALF:
                nc.scalar.copy(
                    out=dst[:, split:HALF, :].rearrange("p (n i) t -> p n t i", i=4),
                    in_=src[:, :, split:HALF].rearrange("p t (n i) -> p n t i", i=4),
                )

        def quantize_c(h, g):
            c_codes[h, g] = keep.tile([P, HALF], U32, name="c_codes%d%d" % (h, g), align_bytes=64)
            c_plane[h, g] = keep.tile([P, HALF], U8, name="c_plane%d%d" % (h, g), align_bytes=64)
            nc.vector.quantize_mx(
                out=c_codes[h, g][:].bitcast(FP8X4),
                scales=c_plane[h, g][:],
                in_=c_grouped[h, g][:].rearrange("p n t -> p (n t)"),
            )

        acc = {}

        def mx_pass(unit, part, g, start=False, stop=False):
            h, t = UNITS[unit]
            if start:
                acc[unit] = bank(unit if unit < WAVE else (unit - WAVE) % ACC_BANKS)
            cols = slice(h * HALF, (h + 1) * HALF)
            if part == "a":
                rhs, rhs_scale = a[h][:, g, :].bitcast(FP4X4), a_plane[:, g, cols]
            elif part == "b":
                rhs, rhs_scale = b[h][:, g, :].bitcast(FP8X4), b_plane[:, g, cols]
            else:
                rhs, rhs_scale = c_codes[h, g][:].bitcast(FP8X4), c_plane[h, g][:]
            chunk, within = divmod(t, CHUNK)
            own = slice(within * P, (within + 1) * P)
            if dealt(unit):
                lhs, lhs_scale = states[chunk][:, g, own], states_plane[chunk][:, g, own]
            elif chunk == 0:
                lhs, lhs_scale = psi[chunk][:, g, own], psi_plane_first[:, g, own]
            else:
                lhs, lhs_scale = psi[chunk][:, g, own], psi_plane_rest[:, g, (t - CHUNK) * P : (t - CHUNK + 1) * P]
            nc.tensor.matmul_mx(
                out=acc[unit][:],
                lhsT=lhs.bitcast(FP8X4),
                lhsT_scale=lhs_scale,
                rhs=rhs,
                rhs_scale=rhs_scale,
                start=start,
                stop=stop,
            )

        def multiply(unit):
            order = [(part, g) for part in "abc" for g in range(GROUPS)]
            for n, (part, g) in enumerate(order):
                mx_pass(unit, part, g, start=(n == 0), stop=(n == len(order) - 1))

        y_pair, y_words = {}, {}

        def finish(unit):
            h, t = UNITS[unit]
            factor = rate_col[:, int(dealt(unit)), t : t + 1]
            square = work.tile([P, HALF], F32, name="square", bufs=8)
            nc.scalar.activation(out=square[:], in_=acc[unit][:], func=ACT.Square)
            y_words[unit] = work.tile([P, 2, P, 2], BF16, name="y_words", bufs=10, align_bytes=64)
            nc.vector.tensor_scalar(
                out=y_words[unit][:],
                in0=square[:].rearrange("m (p u e) -> m u p e", u=2, e=2),
                scalar1=factor,
                scalar2=None,
                op0=ALU.mult,
            )
            if unit % 2 == 0:
                y_pair[unit // 2] = work.tile([P, 2, HALF], F32, name="y_pair", bufs=6)
            nc.vector.tensor_scalar(
                out=y_pair[unit // 2][:, unit % 2, :],
                in0=square[:],
                scalar1=factor,
                scalar2=None,
                op0=ALU.mult,
            )

        def finish_last(unit):
            h, t = UNITS[unit]
            factor = rate_col[:, 0, t : t + 1]
            square = work.tile([P, HALF], F32, name="square", bufs=8)
            halves = square[:].rearrange("m (u p e) -> m u p e", u=2, e=2)
            y_words[unit] = work.tile([P, 2, P, 2], BF16, name="y_words", bufs=10, align_bytes=64)
            for u in range(2):
                nc.scalar.activation(
                    out=halves[:, u],
                    in_=acc[unit][:].rearrange("m (p u e) -> m u p e", u=2, e=2)[:, u],
                    func=ACT.Square,
                )
                nc.vector.tensor_scalar(
                    out=y_words[unit][:, u], in0=halves[:, u], scalar1=factor, scalar2=None, op0=ALU.mult
                )
            nc.vector.tensor_scalar(
                out=y_pair[unit // 2][:, unit % 2, :].rearrange("m (p u e) -> m p u e", u=2, e=2),
                in0=square[:].rearrange("m (u p e) -> m p u e", u=2, e=2),
                scalar1=factor,
                scalar2=None,
                op0=ALU.mult,
            )

        def store_y(first, count):
            h, t = UNITS[first]
            rows = out_0[t * P : (t + count) * P, h * HALF : (h + 1) * HALF]
            nc.sync.dma_start(
                out=rows.rearrange("(t p) n -> p t n", p=P),
                in_=y_pair[first // 2][:, first % 2 : first % 2 + count, :],
            )

        def store_dealt_y(first):
            h, t = UNITS[first]
            chunk, within = divmod(t, CHUNK)
            rows = out_0[chunk * CHUNK * P : (chunk + 1) * CHUNK * P, h * HALF : (h + 1) * HALF]
            nc.sync.dma_start(
                out=rows.rearrange("(p t) n -> p t n", t=CHUNK)[:, within : within + 2, :],
                in_=y_pair[first // 2][:],
            )

        blocks, dealt_src, waiting = {}, {}, {}

        def turn_blocks(unit):
            if unit % 2 == 0:
                blocks[unit // 2] = work.tile([P, 2, 2 * P], F32, name="blocks", bufs=3, align_bytes=64)
            nc.vector.transpose(
                out=blocks[unit // 2][:, unit % 2, :],
                in_=y_words[unit][:].rearrange("m u p e -> m (u p e)").bitcast(F32),
            )

        def gather_blocks(first):
            within = first % CHUNK
            if within == 0:
                dealt_src[first // CHUNK] = work.tile([P, CHUNK * GROUP], BF16, name="dealt_src", bufs=2, align_bytes=64)
            dst = dealt_src[first // CHUNK][:].bitcast(F32).rearrange("a (x t u) -> a x t u", t=CHUNK, u=2)
            nc.scalar.copy(
                out=dst[:, :, within : within + 2, :], in_=blocks[first // 2][:].rearrange("a t (u x) -> a x t u", u=2)
            )

        def dealt_planes(first):
            h, t = UNITS[first]
            for s in range(4):
                nc.vector.quantize_mx(
                    out=y_codes[h][:, (t + s) * P : (t + s + 1) * P].bitcast(FP8X4),
                    scales=dealt_plane[h][4 * s : P, t // CHUNK - 1, :],
                    in_=dealt_src[first // CHUNK][:, s * GROUP : (s + 1) * GROUP],
                )
            for s in range(4):
                dst = out_1[h, 32 * s : 32 * s + 32, t * P : (t + CHUNK) * P, :]
                nc.sync.dma_start(
                    out=dst.rearrange("a (q m) t -> q a (m t)", q=4).bitcast(I32),
                    in_=y_codes[h][:, (t + s) * P : (t + s + 1) * P].bitcast(I32),
                )
            count = t // CHUNK
            if (h, count + 1) not in DEALT:
                for n, q in enumerate((0, 2, 1, 3)):
                    waiting.setdefault(first + CHUNK + max(0, 2 * n - 1), []).append((h, q, count))

        def store_waiting_scales(unit):
            for h, q, count in waiting.get(unit, []):
                dst = out_2[h, :, CHUNK * P : (count + 1) * CHUNK * P].rearrange("j (c q m) -> q j c m", q=4, m=P)[q]
                nc.sync.dma_start(out=dst.bitcast(I32), in_=dealt_plane[h][32 * q : 32 * q + 16, 0:count, :].bitcast(I32))

        dealt_plane = [
            keep.tile([P, CHUNKS - 1, P], U8, name="dealt_plane%d" % h, align_bytes=64) for h in range(HALVES)
        ]
        y_codes = [keep.tile([P, T], U32, name="y_codes%d" % h, align_bytes=64) for h in range(HALVES)]
        y_plane = [keep.tile([P, T], U8, name="y_plane%d" % h, align_bytes=64) for h in range(HALVES)]
        turned, grouped = {}, {}

        def turn(first, count, index):
            turned[first] = bank(index)
            view = turned[first][:].rearrange("p (t u m) -> p t u m", u=2, m=P)
            for n in range(count):
                words = y_words[first + n][:].rearrange("m u p e -> m (u p e)").bitcast(F32)
                for u in range(2):
                    nc.tensor.transpose(view[:, n, u, :], words[:, u * P : (u + 1) * P], identity[:])

        def gather(first, count, dst, offset, engine_copy):
            view = turned[first][:, 0 : count * 2 * P].rearrange("p (t u m) -> p t m u", u=2, m=P)
            words = dst[:].bitcast(F32)[:, offset * 2 * P : (offset + count) * 2 * P]
            engine_copy(out=words.rearrange("p (t m u) -> p t m u", u=2, m=P), in_=view)

        def quantize_y(first, count, src, offset=0):
            h, t = UNITS[first]
            cols = slice(t * P, (t + count) * P)
            nc.vector.quantize_mx(
                out=y_codes[h][:, cols].bitcast(FP8X4),
                scales=y_plane[h][:, cols],
                in_=src[:, offset * GROUP : (offset + count) * GROUP],
            )

        def store_codes(first, count, queue):
            h, t = UNITS[first]
            dst = out_1[h].rearrange("p m t -> p (m t)")[:, t * P * PACK : (t + count) * P * PACK]
            queue.dma_start(out=dst.bitcast(I32), in_=y_codes[h][:, t * P : (t + count) * P].bitcast(I32))

        def store_scales(h, t, count, queues):
            cols = slice(t * P, (t + count) * P)
            for q in range(4):
                queues[q % len(queues)].dma_start(
                    out=out_2[h, 4 * q : 4 * q + 4, cols].bitcast(I32),
                    in_=y_plane[h][32 * q : 32 * q + 4, cols].bitcast(I32),
                )

        def planes(first, count):
            src = work.tile([P, CHUNK * GROUP], BF16, name="grouped", bufs=2, align_bytes=64)
            for pair in range(count // 2):
                gather(first + 2 * pair, 2, src, 2 * pair, nc.scalar.copy)
            return src

        units = len(UNITS)

        def after(unit):
            if unit > 0 and dealt(unit - 1) and unit % CHUNK == 0:
                gather_blocks(unit - 2)
                dealt_planes(unit - CHUNK)
            if unit == units - 1:
                finish_last(unit)
            else:
                finish(unit)
            if dealt(unit):
                turn_blocks(unit)
                if unit % 2 == 1:
                    store_dealt_y(unit - 1)
                if unit % CHUNK == 2:
                    gather_blocks(unit - 2)
            elif unit >= units - 2:
                store_y(unit, 1)
            elif unit % 2 == 1:
                store_y(unit - 1, 2)
            store_waiting_scales(unit)

        interleave_c(0, 0)
        quantize_c(0, 0)
        for first, last in ((0, CHUNK), (CHUNK, WAVE)):
            for unit in range(first, last):
                mx_pass(unit, "c", 0, start=True)
            for unit in range(first, last):
                for g in range(GROUPS):
                    mx_pass(unit, "a", g)
        nc.scalar.copy(out=rate_rows32[:], in_=rate_rows[:])
        rate_bank = bank(7)
        nc.tensor.transpose(rate_bank[:, 0:P], rate_rows32[:], identity[:])
        nc.scalar.copy(out=rate_col[:, 0, :], in_=rate_bank[:, 0:TILES])
        for unit in range(WAVE):
            for g in range(GROUPS):
                mx_pass(unit, "b", g)
        for h, g in ((0, 1), (1, 0), (1, 1)):
            interleave_c(h, g)
            quantize_c(h, g)
        for unit in range(WAVE):
            mx_pass(unit, "c", 1, stop=True)
            after(unit)

        runs = {8: 0, 10: 4, 13: 8, 17: 12, 20: 16}
        for unit in range(WAVE, units):
            multiply(unit)
            if unit in runs:
                turn(runs[unit], 2, 7)
                turn(runs[unit] + 2, 2, 6)
            if unit == units - 2:
                turn(units - 4, 2, 6)
            if unit == units - 1:
                turn(units - 2, 1, 7)
                last_src = work.tile([P, CHUNK * GROUP], BF16, name="grouped", bufs=2, align_bytes=64)
                gather(units - 2, 1, last_src, 0, nc.vector.tensor_copy)
            after(unit)
            if unit in runs:
                src = planes(runs[unit], CHUNK)
                quantize_y(runs[unit], CHUNK, src)
                store_codes(runs[unit], CHUNK, nc.sync)
                if runs[unit] == 8:
                    store_scales(0, 0, TILES, [nc.sync])
                if runs[unit] == 16:
                    store_scales(1, 0, TILES - CHUNK, [nc.sync])
            if unit == units - 2:
                src = planes(units - 4, 2)
                quantize_y(units - 4, 2, src)
                store_codes(units - 4, 2, nc.sync)
        quantize_y(units - 2, 1, last_src)
        turn(units - 1, 1, 6)
        gather(units - 1, 1, last_src, 1, nc.scalar.copy)
        quantize_y(units - 1, 1, last_src, 1)
        store_codes(units - 2, 2, nc.scalar)
        store_scales(1, TILES - CHUNK, CHUNK, [nc.sync, nc.scalar])
